import numpy as np
CORES = [16,17,18,19,150,151]
N = 6
RM, R, T = 262144, 4096, 2048
def entries(a): return a.T.reshape(-1)
def pack(v, P): return np.ascontiguousarray(np.asarray(v, np.int32).reshape(-1, P).T)
def lists(rng, how):
    M = rng.integers(0, N * R, N * RM)
    I = rng.integers(0, N * RM, (N, T))
    if how == "alike": I[:] = rng.integers(0, N * RM, (N, 1)); I[N // 2:] = I[-1, 0]
    if how == "edge":
        en = np.concatenate([RM * np.arange(N), RM * np.arange(N) + RM - 1]); M[en] = rng.permutation(np.concatenate([R * np.arange(N), R * np.arange(N) + R - 1]))
        I = en[rng.integers(0, 2 * N, (N, T))]; I[:, 0] = rng.permutation(en[:N]); I[:, T - 1] = rng.permutation(en[N:])
    if how == "hotrank": I = RM * int(rng.integers(N)) + rng.integers(0, RM, (N, T)); M[I.reshape(-1)] = R * int(rng.integers(N)) + rng.integers(0, R, N * T)
    if how == "cross":
        a = rng.integers(1, N, (N, T)); b = 1 + (a - 1 + rng.integers(1, N - 1, (N, T))) % (N - 1); me = np.arange(N)[:, None]
        I = RM * ((me + a) % N) + T * me + np.arange(T)[None, :]; M[I.reshape(-1)] = (R * ((me + b) % N) + rng.integers(0, R, (N, T))).reshape(-1)
    if how == "fold": M = rng.integers(0, N * R, 16)[rng.integers(0, 16, N * RM)]
    return {"mp": np.stack([pack(m, 16) for m in M.reshape(N, RM)]), "idx": np.stack([pack(i, 16) for i in I])}
def setup_inputs(rng):
    return dict({"tab": rng.standard_normal((N, 128, R), dtype=np.float32)}, **lists(rng, "uniform"))
def setup_inputs_alike(rng):
    d = setup_inputs(rng); d.update(lists(rng, "alike"))
    for k in ("tab",): d[k] = (d[k].astype(np.float32) * 1048576.0).astype(d[k].dtype)
    return d
def setup_inputs_cross(rng):
    d = setup_inputs(rng); d.update(lists(rng, "cross"))
    for k in ("tab",): d[k] = (d[k].astype(np.float32) * (1 / 1024.0)).astype(d[k].dtype)
    return d
def setup_inputs_edge(rng):
    d = setup_inputs(rng); d.update(lists(rng, "edge"))
    return d
def setup_inputs_fold(rng):
    d = setup_inputs(rng); d.update(lists(rng, "fold"))
    return d
def setup_inputs_hotrank(rng):
    d = setup_inputs(rng); d.update(lists(rng, "hotrank"))
    return d
def check_inputs(x):
    bad = []
    if x["mp"].min() < 0 or x["mp"].max() >= N * R: bad.append("mp out of range")
    if x["idx"].min() < 0 or x["idx"].max() >= N * RM: bad.append("idx out of range")
    return bad
def reference(tab, mp, idx):
    A = np.concatenate(list(tab), axis=1)
    M = np.concatenate([entries(m) for m in mp])
    return {"y": np.stack([A[:, M[entries(idx[r])]] for r in range(N)])}

@@ -1,0 +1,393 @@
+from concourse.bass import DstId, RemoteDMATransfer
+from concourse.mybir import AluOpType, ActivationFunctionType
+
+OP = AluOpType
+ACT = ActivationFunctionType
+SIM = 256
+_F, _I, _U, _H = "float32", "int32", "uint16", "bfloat16"
+_SB = [("idxi", 32, _I), ("ti", 64, _I), ("si", 32, _I), ("lf", 64, _F), ("ll", 384, _F), ("lu", 192, _U), ("lb", 192, _H),
+       ("mapw", 8192, _I), ("win", 12800, _F), ("bio", 128, _H), ("lsel", 2048, _H), ("dio", 128, _F), ("eio", 128, _F),
+       ("pio", 4, _I), ("rio", 4, _I), ("bas", 16, _F), ("pa_i", 8, _I), ("pcs", 4, _F), ("npc", 4, _F), ("ri5", 4, _I),
+       ("ind", 4, _F), ("ident", 128, _F), ("repm", 768, _F), ("absb", 3072, _F), ("mask", 3072, _H), ("mg", 3072, _F),
+       ("part", 576, _F), ("s3", 288, _F), ("s2", 96, _F), ("ci", 96, _I), ("e1", 96, _I), ("e2", 96, _I), ("loc", 96, _F),
+       ("par", 96, _I), ("mis", 96, _F), ("isb", 16, _F), ("f2", 48, _F), ("lt", 128, _F), ("lt2", 128, _F), ("ou", 384, _U),
+       ("o2", 384, _U), ("hof", 32, _U), ("bco", 1536, _F), ("sv", 2048, _F), ("mgo", 512, _F), ("yo", 2048, _F)]
+_SB += [("w%d" % i, 16, _F) for i in range(1, 10)]
+SCRATCH = {n: ("sbuf", [128, w], d) for n, w, d in _SB}
+SCRATCH.update({"ps_s": ("psum", [128, 3072], _F), "ps_r": ("psum", [128, 512], _F), "ps_t": ("psum", [128, 512], _F)})
+SEMAPHORES = ["v", "p", "s", "gi", "li", "lm", "lt0", "lt1", "lan", "laf", "pan", "lsm", "tb", "tc0", "tc1",
+              "lbm", "hc", "ho", "lp", "lsv", "m0", "m1", "st"]
+
+
+def rank_program(g, core, T, topo):
+    S = T.sem
+    cores = list(T.cores)
+    rank = T.rank_of(core)
+
+    def place(c):
+        return (topo.host(c), topo.chip(c))
+
+    A = [r for r in range(len(cores)) if place(cores[r]) == place(cores[0])]
+    B = [r for r in range(len(cores)) if r not in A]
+    HA = [c for c in range(SIM) if place(c) == place(cores[A[0]]) and topo.die(c) != topo.die(cores[A[0]])][:4]
+    HB = [c for c in range(SIM) if place(c) == place(cores[B[0]]) and topo.die(c) != topo.die(cores[B[0]])][:2]
+    if rank is None and core not in HA and core not in HB:
+        return
+
+    def bits(m):
+        return [b for b in range(16) if (m >> b) & 1]
+
+    def tomask(bs):
+        return sum(1 << b for b in bs)
+
+    onA = place(core) == place(cores[A[0]])
+    near = [cores[r] for r in (A if onA else B) if cores[r] != core][0]
+    ALL = topo.mask(core, near)
+    OFF = topo.mask(core, cores[B[0]] if onA else cores[A[0]])
+    REST = ALL & ~OFF
+    cnt = {"v": 0, "p": 0, "s": 0, "ls": 0}
+    vec, ten, sca = g.vector, g.tensor, g.scalar
+
+    def V(ins):
+        ins.then_inc(S.v, 1)
+        cnt["v"] += 1
+        return cnt["v"]
+
+    def P(ins):
+        ins.then_inc(S.p, 1)
+        cnt["p"] += 1
+        return cnt["p"]
+
+    def vw():
+        vec.wait_ge(S.v, cnt["v"])
+
+    def ts(out, a, s1, op, s2=None, op2=None):
+        if op2 is None:
+            return V(vec.tensor_scalar(out, a, s1, None, op))
+        return V(vec.tensor_scalar(out, a, s1, s2, op, op2))
+
+    def tt(out, a, b, op):
+        return V(vec.tensor_tensor(out, a, b, op))
+
+    def cp(out, a):
+        return V(vec.tensor_copy(out, a))
+
+    def xfer(dests, src, dst, mask, sem):
+        ids = []
+        for d in dests:
+            rid, pid = topo.addr(d, core)
+            ids.append(DstId(rid=rid, pnc=pid))
+        cnt["ls"] += len(bits(mask))
+        return RemoteDMATransfer(dst_ids=ids, dma_engine_mask=mask, remote_sem=sem, srcs=[src], dsts=[dst] * len(ids), alu_op=0)
+
+    def send(*trs):
+        g.remote_dma_fused(list(trs), local_sem=S.lsm)
+
+    if core in HA:
+        k = HA.index(core)
+        e, h = k & 1, k >> 1
+        vec.wait_ge(S.hc, 8)
+        vec.wait_ge(S.ho, len(bits(ALL)))
+        n = cp(T.mgo[:, :], T.win[:, 0:1024].indirect(T.hof[:, 0:32]))
+        g.wait_ge(S.v, n)
+        c0 = 8192 + 512 * (2 + h)
+        send(xfer([cores[B[e]]], T.mgo[:, :], T.win[:, c0:c0 + 512], OFF, S.m1))
+        g.wait_ge(S.lsm, cnt["ls"])
+        return
+
+    isA = rank is not None and rank in A
+    isB = rank is not None and rank in B
+    if isA:
+        pa, h, pt, mate = rank & 1, rank >> 1, rank ^ 1, rank ^ 2
+        tab0 = 512 + 4096 * h
+    elif isB:
+        bi = B.index(rank)
+        tab0 = 4096 * bi
+
+    if rank is not None:
+        g.sync.dma_start(T.idxi[:, 0:16], T.idx[:, :]).then_inc(S.li, 16)
+        sca.dma_start(T.idxi[:, 16:32], T.idx[:, :]).then_inc(S.li, 16)
+
+        def load_map():
+            for k in range(4):
+                q = g.sync if k % 2 == 0 else sca
+                q.dma_start(T.mapw[32 * k:32 * k + 32, :], T.mp[:, :]).then_inc(S.lm, 16)
+
+        def load_tab():
+            g.sync.dma_start(T.win[:, tab0:tab0 + 2048], T.tab[:, 0:2048]).then_inc(S.lt0, 16)
+            sca.dma_start(T.win[:, tab0 + 2048:tab0 + 4096], T.tab[:, 2048:4096]).then_inc(S.lt1, 16)
+        for f in ([load_tab, load_map] if isB else [load_map, load_tab]):
+            f()
+
+    ngi = 2
+    imp = dict(allow_small_or_imprecise_dtypes=True)
+    if rank is not None:
+        g.iota(T.bio[:, :], [[-32, 4], [0, 32]], 0, 1, **imp).then_inc(S.gi, 1)
+        g.iota(T.pio[:, 0:1], [[1, 1]], 0, 1).then_inc(S.gi, 1)
+        g.iota(T.rio[:, :], [[-32, 4]], 0, 1).then_inc(S.gi, 1)
+        g.iota(T.bas[:, :], [[1, 16]], 0, 16, **imp).then_inc(S.gi, 1)
+        ngi += 4
+    g.iota(T.dio[:, :], [[-1, 128]], 0, 1, **imp).then_inc(S.gi, 1)
+    g.iota(T.eio[:, :], [[0, 8], [-1, 16]], 0, 1, **imp).then_inc(S.gi, 1)
+
+    if rank is not None:
+        vec.wait_ge(S.li, 32)
+        ts(T.ti[:, 0:32], T.idxi[:, :], 4, OP.arith_shift_right, 8191, OP.bitwise_and)
+        ts(T.si[:, :], T.idxi[:, :], 15, OP.bitwise_and)
+        ts(T.ti[:, 32:64], T.idxi[:, :], 13, OP.arith_shift_right, 0xFFFFF0, OP.bitwise_and)
+        vw()
+        cp(T.lf[:, 0:32], T.ti[:, 0:32])
+        tt(T.lf[:, 32:64], T.si[:, :], T.ti[:, 32:64], OP.add)
+        vw()
+        own = slice(64 * rank, 64 * rank + 64)
+        V(vec.transpose(T.ll[:, own], T.lf[:, :]))
+        g.wait_ge(S.v, cnt["v"])
+        onr = [r for r in (A if isA else B) if r != rank]
+        ofr = B if isA else A
+        send(xfer([cores[r] for r in onr], T.ll[:, own], T.ll[:, own], REST, S.lan),
+             xfer([cores[r] for r in ofr], T.ll[:, own], T.ll[:, own], OFF, S.laf))
+        for c in range(2):
+            sl = slice(tab0 + 2048 * c, tab0 + 2048 * c + 2048)
+            g.wait_ge(S["lt%d" % c], 16)
+            to = [cores[mate]] if isA else [HB[bi], cores[B[1 - bi]]]
+            send(xfer(to, T.win[:, sl], T.win[:, sl], ALL, S["tc%d" % c]))
+        vec.wait_ge(S.gi, ngi)
+        ts(T.pa_i[:, 0:1], T.pio[:, 0:1], 1, OP.arith_shift_right, 15, OP.bitwise_and)
+        ts(T.pa_i[:, 4:5], T.pio[:, 0:1], 1, OP.bitwise_and)
+        ts(T.ri5[:, :], T.rio[:, :], 5, OP.arith_shift_right)
+        vw()
+        ts(T.pcs[:, 1:2], T.pa_i[:, 4:5], 16.0, OP.mult, float(32 * rank), OP.add)
+        ts(T.ind[:, :], T.ri5[:, :], 0.0, OP.is_equal)
+        vw()
+        tt(T.pcs[:, 0:1], T.pa_i[:, 0:1], T.pcs[:, 1:2], OP.add)
+        vw()
+        ts(T.npc[:, 0:1], T.pcs[:, 0:1], -1.0, OP.mult)
+        for x in range(16):
+            ts(T.lsel[:, 128 * x:128 * x + 128], T.bio[:, :], float(x), OP.is_equal)
+
+        vc, pb, pos = {}, {}, {}
+
+        def conv(r):
+            cp(T.lb[:, 32 * r:32 * r + 32], T.ll[:, 64 * r + 32:64 * r + 64])
+            vc[r] = cp(T.lu[:, 32 * r:32 * r + 32], T.ll[:, 64 * r:64 * r + 32])
+
+        def bcast(r):
+            ten.wait_ge(S.v, vc[r])
+            for x in range(16):
+                ins = ten.matmul(T.ps_s[:, 512 * r + x:512 * r + 512:16], T.lsel[:, 128 * x:128 * x + 128],
+                                 T.lb[:, 32 * r:32 * r + 32], True, True)
+            pb[r] = P(ins)
+
+        def look(r):
+            b = slice(512 * r, 512 * r + 512)
+            if pos[r] % 2:
+                sca.wait_ge(S.p, pb[r])
+                sca.wait_ge(S.v, vc[r])
+                sca.activation(T.absb[:, b], T.ps_s[:, b], ACT.Abs, bias=T.npc[:, 0:1], scale=1.0).then_inc(S.s, 1)
+                sca.wait_ge(S.s, cnt["s"] + 1)
+                sca.activation(T.mask[:, b], T.absb[:, b], ACT.Relu, bias=1.0, scale=-1.0).then_inc(S.s, 1)
+                cnt["s"] += 2
+                vec.wait_ge(S.s, cnt["s"])
+            else:
+                vec.wait_ge(S.p, pb[r])
+                ts(T.mask[:, b], T.ps_s[:, b], T.pcs[:, 0:1], OP.is_equal)
+            vec.wait_ge(S.lm, 64)
+            vw()
+            return tt(T.mg[:, b], T.mapw[:, :].indirect(T.lu[:, 32 * r:32 * r + 32]), T.mask[:, b], OP.mult)
+
+        def reduce(r, n):
+            ten.wait_ge(S.v, n)
+            for bb in range(4):
+                ins = ten.matmul(T.ps_r[:, 16 * r + bb:16 * r + 16:4], T.mg[:, 512 * r + 128 * bb:512 * r + 128 * bb + 128],
+                                 T.ind[:, :], True, True)
+            P(ins)
+
+        for i, r in enumerate([rank] + onr + ofr):
+            pos[r] = i
+        conv(rank)
+        bcast(rank)
+        vec.wait_ge(S.lan, len(bits(REST)) * len(onr))
+        for r in onr:
+            conv(r)
+        for r in onr:
+            bcast(r)
+        reduce(rank, look(rank))
+        vec.wait_ge(S.laf, len(bits(OFF)) * len(ofr))
+        for r in ofr:
+            conv(r)
+        pend = list(ofr)
+        bcast(pend.pop(0))
+        for r in onr + ofr:
+            n = look(r)
+            if pend:
+                bcast(pend.pop(0))
+            reduce(r, n)
+        vec.wait_ge(S.p, cnt["p"])
+        mine = slice(96 * rank, 96 * rank + 96)
+        cp(T.part[:, mine], T.ps_r[:, 0:96])
+        g.wait_ge(S.v, cnt["v"])
+        send(xfer([cores[r] for r in onr] + (HB if isB else []), T.part[:, mine], T.part[:, mine], REST, S.pan),
+             xfer([cores[r] for r in ofr] + (HB if isA else []), T.part[:, mine], T.part[:, mine], OFF, S.pan))
+    else:
+        k = HB.index(core)
+        for c in range(2):
+            sl = slice(4096 * k + 2048 * c, 4096 * k + 2048 * c + 2048)
+            g.wait_ge(S["tc%d" % c], len(bits(ALL)))
+            send(xfer([HB[1 - k]], T.win[:, sl], T.win[:, sl], ALL, S.tb))
+        vec.wait_ge(S.gi, ngi)
+
+    ts(T.ident[:, :], T.dio[:, :], 0.0, OP.is_equal)
+    for r in range(6):
+        ts(T.repm[:, 128 * r:128 * r + 128], T.eio[:, :], float(16 * r), OP.is_equal)
+
+    vec.wait_ge(S.pan, 8 * (len(cores) - (0 if rank is None else 1)))
+    vw()
+    tt(T.s3[:, :], T.part[:, 0:288], T.part[:, 288:576], OP.add)
+    vw()
+    tt(T.s2[:, :], T.s3[:, 0:96], T.s3[:, 96:192], OP.add)
+    vw()
+    tt(T.ci[:, :], T.s2[:, :], T.s3[:, 192:288], OP.add)
+    vw()
+    if isA:
+        ts(T.e1[:, :], T.ci[:, :], 1, OP.arith_shift_right, 4096, OP.bitwise_and)
+        ts(T.e2[:, :], T.ci[:, :], 4095, OP.bitwise_and)
+        vw()
+        tt(T.loc[:, :], T.e1[:, :], T.e2[:, :], OP.add)
+    else:
+        ts(T.e2[:, :], T.ci[:, :], 8191, OP.bitwise_and)
+        vw()
+        cp(T.loc[:, :], T.e2[:, :])
+
+    def turn(src, rows, ps):
+        ten.wait_ge(S.v, cnt["v"])
+        return P(ten.matmul(ps[0:rows, 0:128], src, T.ident[:, :], True, True))
+
+    def spread(lt, rows, blocks, col):
+        for i, b in enumerate(blocks):
+            ins = ten.matmul(T.ps_s[:, col + 128 * i:col + 128 * i + 128], T.repm[0:rows, 128 * b:128 * b + 128],
+                             lt[0:rows, :], True, True)
+        return P(ins)
+
+    def store(c, n):
+        q = g.sync if c % 2 == 0 else sca
+        q.wait_ge(S.v, n)
+        q.dma_start(T.y[:, 512 * c:512 * c + 512], T.yo[:, 512 * c:512 * c + 512]).then_inc(S.st, 16)
+
+    n1 = turn(T.loc[:, :], 96, T.ps_t)
+    if rank is not None:
+        po = slice(16 * rank, 16 * rank + 16)
+    if isA:
+        lbn = B[pa]
+        pl = slice(16 * lbn, 16 * lbn + 16)
+        ts(T.par[:, :], T.ci[:, :], 12, OP.arith_shift_right, 1, OP.bitwise_and)
+        vec.wait_ge(S.p, n1)
+        cp(T.lt[0:96, :], T.ps_t[0:96, 0:128])
+        ten.wait_ge(S.v, cnt["v"])
+        nB = spread(T.lt, 96, B, 0)
+        nP = spread(T.lt, 96, [pt], 512)
+        vw()
+        ts(T.mis[:, :], T.par[:, :], float(pa), OP.not_equal)
+        vec.wait_ge(S.p, nB)
+        cp(T.ou[:, 0:256], T.ps_s[:, 0:256])
+        for nm_, ct in (("lt0", 16), ("lt1", 16), ("tc0", 16), ("tc1", 16)):
+            vec.wait_ge(S[nm_], ct)
+        vw()
+        tw = slice(512, 8704)
+        for i, (l, m) in enumerate([(pt & 1, 32 * h), (0, 64 + 32 * h), (1, 64 + 32 * h)]):
+            cp(T.bco[:, 512 * i:512 * i + 512], T.win[:, tw].indirect(T.ou[:, 128 * l + m:128 * l + m + 32]))
+        g.wait_ge(S.v, cnt["v"])
+        ab = bits(ALL)
+        hw = slice(512 * pa, 512 * pa + 512)
+        send(xfer([cores[pt]], T.bco[:, 0:512], T.win[:, 0:512], tomask(ab[0:8]), S.lbm),
+             xfer([HA[2 * h]], T.bco[:, 512:1024], T.win[:, hw], tomask(ab[8:12]), S.hc),
+             xfer([HA[2 * h + 1]], T.bco[:, 1024:1536], T.win[:, hw], tomask(ab[12:16]), S.hc))
+        ts(T.isb[:, :], T.ci[:, po], 16384.0, OP.is_ge)
+        ts(T.w1[:, :], T.bas[:, :], 8192.0, OP.add)
+        ts(T.w5[:, :], T.bas[:, :], float(-512 * h - 512), OP.add)
+        ts(T.w8[:, :], T.par[:, pl], 512.0, OP.mult, float(-512 * (2 + h)), OP.add)
+        vw()
+        tt(T.f2[:, 32:48], T.w8[:, :], T.bas[:, :], OP.add)
+        tt(T.w6[:, :], T.w5[:, :], T.loc[:, pl], OP.subtract)
+        tt(T.w2[:, :], T.w1[:, :], T.loc[:, po], OP.subtract)
+        tt(T.w3[:, :], T.mis[:, po], T.isb[:, :], OP.max)
+        ts(T.w9[:, :], T.isb[:, :], 2048.0, OP.mult)
+        vw()
+        tt(T.w7[:, :], T.w6[:, :], T.mis[:, pl], OP.mult)
+        tt(T.w4[:, :], T.w2[:, :], T.w3[:, :], OP.mult)
+        ts(T.w5[:, :], T.loc[:, pl], 512.0, OP.add)
+        tt(T.w8[:, :], T.loc[:, po], T.w9[:, :], OP.add)
+        vw()
+        tt(T.f2[:, 16:32], T.w5[:, :], T.w7[:, :], OP.add)
+        tt(T.f2[:, 0:16], T.w8[:, :], T.w4[:, :], OP.add)
+        n2 = turn(T.f2[:, :], 48, T.ps_r)
+        vec.wait_ge(S.p, nP)
+        cp(T.ou[:, 256:384], T.ps_s[:, 512:640])
+        vec.wait_ge(S.p, n2)
+        cp(T.lt2[0:48, :], T.ps_r[0:48, 0:128])
+        ten.wait_ge(S.v, cnt["v"])
+        n3 = spread(T.lt2, 48, [0, 1, 2], 1024)
+        vw()
+        cp(T.sv[:, 0:1024], T.win[:, tw].indirect(T.ou[:, 256:320]))
+        vec.wait_ge(S.p, n3)
+        cp(T.o2[:, :], T.ps_s[:, 1024:1408])
+        vw()
+        nho = cp(T.hof[:, :], T.o2[:, 320 + 32 * h:352 + 32 * h])
+        cp(T.sv[:, 1024:2048], T.win[:, tw].indirect(T.ou[:, 320:384]))
+        vec.wait_ge(S.lbm, 8)
+        nm = cp(T.mgo[:, :], T.win[:, 0:8704].indirect(T.o2[:, 128 + 32 * h:160 + 32 * h]))
+        g.wait_ge(S.v, nho)
+        send(xfer([HA[rank]], T.hof[:, :], T.hof[:, :], ALL, S.ho))
+        send(xfer([cores[pt]], T.sv[:, 0:1024], T.win[:, 8704:9728], ALL, S.lp))
+        g.wait_ge(S.v, nm)
+        c0 = 8192 + 512 * h
+        send(xfer([cores[lbn]], T.mgo[:, :], T.win[:, c0:c0 + 512], OFF, S.m0))
+        send(xfer([cores[pt]], T.sv[:, 1024:2048], T.win[:, 9728:10752], ALL, S.lp))
+        vec.wait_ge(S.lp, 32)
+        vec.wait_ge(S.lsv, 16)
+        for c in range(4):
+            store(c, cp(T.yo[:, 512 * c:512 * c + 512], T.win[:, 512:12800].indirect(T.o2[:, 32 * c:32 * c + 32])))
+    else:
+        s = B.index(rank) if isB else 2 + HB.index(core)
+        vec.wait_ge(S.p, n1)
+        cp(T.lt[0:96, :], T.ps_t[0:96, 0:128])
+        ten.wait_ge(S.v, cnt["v"])
+        vec.wait_ge(S.p, spread(T.lt, 96, [A[s]], 0))
+        cp(T.ou[:, 0:128], T.ps_s[:, 0:128])
+        if isB:
+            vec.wait_ge(S.lt0, 16)
+            vec.wait_ge(S.lt1, 16)
+        else:
+            vec.wait_ge(S.tb, 32)
+        vec.wait_ge(S.tc0, 16)
+        vec.wait_ge(S.tc1, 16)
+        vw()
+        for c in range(2):
+            sc = slice(1024 * c, 1024 * c + 1024)
+            n = cp(T.sv[:, sc], T.win[:, 0:8192].indirect(T.ou[:, 64 * c:64 * c + 64]))
+            g.wait_ge(S.v, n)
+            send(xfer([cores[A[s]]], T.sv[:, sc], T.win[:, 10752 + 1024 * c:11776 + 1024 * c], OFF, S.lsv))
+        if isB:
+            ts(T.isb[:, :], T.ci[:, po], 16384.0, OP.is_ge)
+            ts(T.w1[:, :], T.bas[:, :], 8192.0, OP.add)
+            vw()
+            tt(T.w2[:, :], T.loc[:, po], T.w1[:, :], OP.subtract)
+            vw()
+            tt(T.w3[:, :], T.w2[:, :], T.isb[:, :], OP.mult)
+            vw()
+            tt(T.f2[:, 0:16], T.w3[:, :], T.w1[:, :], OP.add)
+            n2 = turn(T.f2[:, 0:16], 16, T.ps_r)
+            vec.wait_ge(S.p, n2)
+            cp(T.lt2[0:16, :], T.ps_r[0:16, 0:128])
+            ten.wait_ge(S.v, cnt["v"])
+            vec.wait_ge(S.p, spread(T.lt2, 16, [0], 1024))
+            cp(T.o2[:, 0:128], T.ps_s[:, 1024:1152])
+            vw()
+            for c in range(4):
+                if c % 2 == 0:
+                    vec.wait_ge(S["m%d" % (c // 2)], 16)
+                w = 9216 if c < 2 else 10240
+                store(c, cp(T.yo[:, 512 * c:512 * c + 512], T.win[:, 0:w].indirect(T.o2[:, 32 * c:32 * c + 32])))
+    if rank is not None:
+        g.wait_ge(S.st, 64)
+    g.wait_ge(S.v, cnt["v"])
+    g.wait_ge(S.lsm, cnt["ls"])

@@ -16,7 +16,7 @@ _SB += [("w%d" % i, 16, _F) for i in range(1, 10)]
 SCRATCH = {n: ("sbuf", [128, w], d) for n, w, d in _SB}
 SCRATCH.update({"ps_s": ("psum", [128, 3072], _F), "ps_r": ("psum", [128, 512], _F), "ps_t": ("psum", [128, 512], _F)})
 SEMAPHORES = ["v", "p", "s", "gi", "li", "lm", "lt0", "lt1", "lan", "laf", "pan", "lsm", "tb", "tc0", "tc1",
-              "lbm", "hc", "ho", "lp", "lsv", "m0", "m1", "st"]
+              "lbm", "hc", "ho", "lp", "lsv0", "lsv1", "lsv2", "lsv3", "m0", "m1", "st"]
 
 
 def rank_program(g, core, T, topo):
@@ -104,20 +104,15 @@ def rank_program(g, core, T, topo):
         bi = B.index(rank)
         tab0 = 4096 * bi
 
+    def load_map(k):
+        q = g.sync if k % 2 == 0 else sca
+        q.dma_start(T.mapw[32 * k:32 * k + 32, :], T.mp[:, :]).then_inc(S.lm, 16)
+
     if rank is not None:
         g.sync.dma_start(T.idxi[:, 0:16], T.idx[:, :]).then_inc(S.li, 16)
         sca.dma_start(T.idxi[:, 16:32], T.idx[:, :]).then_inc(S.li, 16)
-
-        def load_map():
-            for k in range(4):
-                q = g.sync if k % 2 == 0 else sca
-                q.dma_start(T.mapw[32 * k:32 * k + 32, :], T.mp[:, :]).then_inc(S.lm, 16)
-
-        def load_tab():
-            g.sync.dma_start(T.win[:, tab0:tab0 + 2048], T.tab[:, 0:2048]).then_inc(S.lt0, 16)
-            sca.dma_start(T.win[:, tab0 + 2048:tab0 + 4096], T.tab[:, 2048:4096]).then_inc(S.lt1, 16)
-        for f in ([load_tab, load_map] if isB else [load_map, load_tab]):
-            f()
+        load_map(0)
+        load_map(1)
 
     ngi = 2
     imp = dict(allow_small_or_imprecise_dtypes=True)
@@ -146,11 +141,18 @@ def rank_program(g, core, T, topo):
         ofr = B if isA else A
         send(xfer([cores[r] for r in onr], T.ll[:, own], T.ll[:, own], REST, S.lan),
              xfer([cores[r] for r in ofr], T.ll[:, own], T.ll[:, own], OFF, S.laf))
-        for c in range(2):
+        for q in (g.sync, sca):
+            q.wait_ge(S.v, cnt["v"])
+        load_map(2)
+        load_map(3)
+        g.sync.dma_start(T.win[:, tab0:tab0 + 2048], T.tab[:, 0:2048]).then_inc(S.lt0, 16)
+        sca.dma_start(T.win[:, tab0 + 2048:tab0 + 4096], T.tab[:, 2048:4096]).then_inc(S.lt1, 16)
+
+        def tables(c, to):
             sl = slice(tab0 + 2048 * c, tab0 + 2048 * c + 2048)
-            g.wait_ge(S["lt%d" % c], 16)
-            to = [cores[mate]] if isA else [HB[bi], cores[B[1 - bi]]]
             send(xfer(to, T.win[:, sl], T.win[:, sl], ALL, S["tc%d" % c]))
+        g.wait_ge(S.lt0, 16)
+        tables(0, [cores[mate]] if isA else [HB[bi]])
         vec.wait_ge(S.gi, ngi)
         ts(T.pa_i[:, 0:1], T.pio[:, 0:1], 1, OP.arith_shift_right, 15, OP.bitwise_and)
         ts(T.pa_i[:, 4:5], T.pio[:, 0:1], 1, OP.bitwise_and)
@@ -165,7 +167,7 @@ def rank_program(g, core, T, topo):
         for x in range(16):
             ts(T.lsel[:, 128 * x:128 * x + 128], T.bio[:, :], float(x), OP.is_equal)
 
-        vc, pb, pos = {}, {}, {}
+        vc, pb, ms = {}, {}, {}
 
         def conv(r):
             cp(T.lb[:, 32 * r:32 * r + 32], T.ll[:, 64 * r + 32:64 * r + 64])
@@ -178,56 +180,65 @@ def rank_program(g, core, T, topo):
                                  T.lb[:, 32 * r:32 * r + 32], True, True)
             pb[r] = P(ins)
 
-        def look(r):
+        def onehot(r, on_scalar):
             b = slice(512 * r, 512 * r + 512)
-            if pos[r] % 2:
+            if on_scalar:
                 sca.wait_ge(S.p, pb[r])
                 sca.wait_ge(S.v, vc[r])
                 sca.activation(T.absb[:, b], T.ps_s[:, b], ACT.Abs, bias=T.npc[:, 0:1], scale=1.0).then_inc(S.s, 1)
                 sca.wait_ge(S.s, cnt["s"] + 1)
                 sca.activation(T.mask[:, b], T.absb[:, b], ACT.Relu, bias=1.0, scale=-1.0).then_inc(S.s, 1)
                 cnt["s"] += 2
-                vec.wait_ge(S.s, cnt["s"])
+                ms[r] = cnt["s"]
             else:
                 vec.wait_ge(S.p, pb[r])
                 ts(T.mask[:, b], T.ps_s[:, b], T.pcs[:, 0:1], OP.is_equal)
-            vec.wait_ge(S.lm, 64)
-            vw()
-            return tt(T.mg[:, b], T.mapw[:, :].indirect(T.lu[:, 32 * r:32 * r + 32]), T.mask[:, b], OP.mult)
 
-        def reduce(r, n):
+        def look(r):
+            b = slice(512 * r, 512 * r + 512)
+            if r in ms:
+                vec.wait_ge(S.s, ms[r])
+            n = tt(T.mg[:, b], T.mapw[:, :].indirect(T.lu[:, 32 * r:32 * r + 32]), T.mask[:, b], OP.mult)
             ten.wait_ge(S.v, n)
             for bb in range(4):
                 ins = ten.matmul(T.ps_r[:, 16 * r + bb:16 * r + 16:4], T.mg[:, 512 * r + 128 * bb:512 * r + 128 * bb + 128],
                                  T.ind[:, :], True, True)
             P(ins)
 
-        for i, r in enumerate([rank] + onr + ofr):
-            pos[r] = i
+        order = [rank] + onr + ofr
         conv(rank)
         bcast(rank)
+        onehot(rank, False)
         vec.wait_ge(S.lan, len(bits(REST)) * len(onr))
         for r in onr:
             conv(r)
         for r in onr:
             bcast(r)
-        reduce(rank, look(rank))
+        for r in onr:
+            onehot(r, order.index(r) % 2 == 1)
         vec.wait_ge(S.laf, len(bits(OFF)) * len(ofr))
         for r in ofr:
             conv(r)
-        pend = list(ofr)
-        bcast(pend.pop(0))
-        for r in onr + ofr:
-            n = look(r)
-            if pend:
-                bcast(pend.pop(0))
-            reduce(r, n)
+        for r in ofr:
+            bcast(r)
+        for r in ofr:
+            onehot(r, order.index(r) % 2 == 1)
+        vec.wait_ge(S.lm, 64)
+        vw()
+        for r in order:
+            look(r)
         vec.wait_ge(S.p, cnt["p"])
         mine = slice(96 * rank, 96 * rank + 96)
         cp(T.part[:, mine], T.ps_r[:, 0:96])
         g.wait_ge(S.v, cnt["v"])
         send(xfer([cores[r] for r in onr] + (HB if isB else []), T.part[:, mine], T.part[:, mine], REST, S.pan),
              xfer([cores[r] for r in ofr] + (HB if isA else []), T.part[:, mine], T.part[:, mine], OFF, S.pan))
+        g.wait_ge(S.lt1, 16)
+        if isA:
+            tables(1, [cores[mate]])
+        else:
+            tables(1, [HB[bi], cores[B[1 - bi]]])
+            tables(0, [cores[B[1 - bi]]])
     else:
         k = HB.index(core)
         for c in range(2):
@@ -343,9 +354,10 @@ def rank_program(g, core, T, topo):
         send(xfer([cores[lbn]], T.mgo[:, :], T.win[:, c0:c0 + 512], OFF, S.m0))
         send(xfer([cores[pt]], T.sv[:, 1024:2048], T.win[:, 9728:10752], ALL, S.lp))
         vec.wait_ge(S.lp, 32)
-        vec.wait_ge(S.lsv, 16)
         for c in range(4):
-            store(c, cp(T.yo[:, 512 * c:512 * c + 512], T.win[:, 512:12800].indirect(T.o2[:, 32 * c:32 * c + 32])))
+            vec.wait_ge(S["lsv%d" % c], 8)
+            store(c, cp(T.yo[:, 512 * c:512 * c + 512],
+                        T.win[:, 512:11264 + 512 * c].indirect(T.o2[:, 32 * c:32 * c + 32])))
     else:
         s = B.index(rank) if isB else 2 + HB.index(core)
         vec.wait_ge(S.p, n1)
@@ -361,11 +373,11 @@ def rank_program(g, core, T, topo):
         vec.wait_ge(S.tc0, 16)
         vec.wait_ge(S.tc1, 16)
         vw()
-        for c in range(2):
-            sc = slice(1024 * c, 1024 * c + 1024)
-            n = cp(T.sv[:, sc], T.win[:, 0:8192].indirect(T.ou[:, 64 * c:64 * c + 64]))
+        for c in range(4):
+            sc = slice(512 * c, 512 * c + 512)
+            n = cp(T.sv[:, sc], T.win[:, 0:8192].indirect(T.ou[:, 32 * c:32 * c + 32]))
             g.wait_ge(S.v, n)
-            send(xfer([cores[A[s]]], T.sv[:, sc], T.win[:, 10752 + 1024 * c:11776 + 1024 * c], OFF, S.lsv))
+            send(xfer([cores[A[s]]], T.sv[:, sc], T.win[:, 10752 + 512 * c:11264 + 512 * c], OFF, S["lsv%d" % c]))
         if isB:
             ts(T.isb[:, :], T.ci[:, po], 16384.0, OP.is_ge)
             ts(T.w1[:, :], T.bas[:, :], 8192.0, OP.add)

@@ -8,14 +8,13 @@ _F, _I, _U, _H = "float32", "int32", "uint16", "bfloat16"
 _SB = [("idxi", 32, _I), ("ti", 64, _I), ("si", 32, _I), ("lf", 64, _F), ("ll", 384, _F), ("lu", 192, _U), ("lb", 192, _H),
        ("mapw", 8192, _I), ("win", 12800, _F), ("bio", 128, _H), ("lsel", 2048, _H), ("dio", 128, _F), ("eio", 128, _F),
        ("pio", 4, _I), ("rio", 4, _I), ("bas", 16, _F), ("pa_i", 8, _I), ("pcs", 4, _F), ("npc", 4, _F), ("ri5", 4, _I),
-       ("ind", 4, _F), ("ident", 128, _F), ("repm", 768, _F), ("absb", 3072, _F), ("mask", 3072, _H), ("mg", 3072, _F),
-       ("part", 576, _F), ("s3", 288, _F), ("s2", 96, _F), ("ci", 96, _I), ("e1", 96, _I), ("e2", 96, _I), ("loc", 96, _F),
-       ("par", 96, _I), ("mis", 96, _F), ("isb", 16, _F), ("f2", 48, _F), ("lt", 128, _F), ("lt2", 128, _F), ("ou", 384, _U),
-       ("o2", 384, _U), ("hof", 32, _U), ("bco", 1536, _F), ("sv", 2048, _F), ("mgo", 512, _F), ("yo", 2048, _F)]
-_SB += [("w%d" % i, 16, _F) for i in range(1, 10)]
+       ("ind", 4, _F), ("ident", 128, _F), ("repm", 384, _F), ("absb", 3072, _F), ("mask", 3072, _H), ("mg", 3072, _F),
+       ("part", 576, _F), ("q", 512, _F), ("ci", 96, _I), ("e1", 96, _I), ("e2", 96, _I),
+       ("loc", 112, _F), ("hp", 16, _I), ("par", 96, _I), ("mis", 96, _F), ("lt", 384, _F), ("ou", 512, _U),
+       ("bco", 1536, _F), ("sv", 2048, _F), ("mgo", 512, _F), ("yo", 2048, _F), ("w", 256, _F)]
 SCRATCH = {n: ("sbuf", [128, w], d) for n, w, d in _SB}
 SCRATCH.update({"ps_s": ("psum", [128, 3072], _F), "ps_r": ("psum", [128, 512], _F), "ps_t": ("psum", [128, 512], _F)})
-SEMAPHORES = ["v", "p", "s", "gi", "li", "lm", "lt0", "lt1", "lan", "laf", "pan", "lsm", "tb", "tc0", "tc1",
+SEMAPHORES = ["v", "p", "s", "gi", "li", "lm", "lm2", "lt0", "lt1", "lan", "laf", "pan", "lsm", "tb", "tc0", "tc1",
               "lbm", "hc", "ho", "lp", "lsv0", "lsv1", "lsv2", "lsv3", "m0", "m1", "st"]
 
 
@@ -37,14 +36,12 @@ def rank_program(g, core, T, topo):
     def bits(m):
         return [b for b in range(16) if (m >> b) & 1]
 
-    def tomask(bs):
-        return sum(1 << b for b in bs)
-
     onA = place(core) == place(cores[A[0]])
     near = [cores[r] for r in (A if onA else B) if cores[r] != core][0]
     ALL = topo.mask(core, near)
     OFF = topo.mask(core, cores[B[0]] if onA else cores[A[0]])
     REST = ALL & ~OFF
+    NALL = len(bits(ALL))
     cnt = {"v": 0, "p": 0, "s": 0, "ls": 0}
     vec, ten, sca = g.vector, g.tensor, g.scalar
 
@@ -72,6 +69,9 @@ def rank_program(g, core, T, topo):
     def cp(out, a):
         return V(vec.tensor_copy(out, a))
 
+    def W(n):
+        return T.w[:, 16 * n:16 * n + 16]
+
     def xfer(dests, src, dst, mask, sem):
         ids = []
         for d in dests:
@@ -86,9 +86,9 @@ def rank_program(g, core, T, topo):
     if core in HA:
         k = HA.index(core)
         e, h = k & 1, k >> 1
-        vec.wait_ge(S.hc, 8)
-        vec.wait_ge(S.ho, len(bits(ALL)))
-        n = cp(T.mgo[:, :], T.win[:, 0:1024].indirect(T.hof[:, 0:32]))
+        vec.wait_ge(S.ho, NALL)
+        vec.wait_ge(S.hc, 2 * NALL)
+        n = cp(T.mgo[:, :], T.win[:, 0:1024].indirect(T.ou[:, 96:128]))
         g.wait_ge(S.v, n)
         c0 = 8192 + 512 * (2 + h)
         send(xfer([cores[B[e]]], T.mgo[:, :], T.win[:, c0:c0 + 512], OFF, S.m1))
@@ -97,22 +97,24 @@ def rank_program(g, core, T, topo):
 
     isA = rank is not None and rank in A
     isB = rank is not None and rank in B
+    CX = 4096 if isA else 2048
     if isA:
         pa, h, pt, mate = rank & 1, rank >> 1, rank ^ 1, rank ^ 2
         tab0 = 512 + 4096 * h
+        lbn = B[pa]
+        pl = slice(16 * lbn, 16 * lbn + 16)
+        pp = slice(16 * pt, 16 * pt + 16)
     elif isB:
         bi = B.index(rank)
         tab0 = 4096 * bi
-
-    def load_map(k):
-        q = g.sync if k % 2 == 0 else sca
-        q.dma_start(T.mapw[32 * k:32 * k + 32, :], T.mp[:, :]).then_inc(S.lm, 16)
+    if rank is not None:
+        po = slice(16 * rank, 16 * rank + 16)
 
     if rank is not None:
         g.sync.dma_start(T.idxi[:, 0:16], T.idx[:, :]).then_inc(S.li, 16)
         sca.dma_start(T.idxi[:, 16:32], T.idx[:, :]).then_inc(S.li, 16)
-        load_map(0)
-        load_map(1)
+        g.sync.dma_start(T.mapw[0:32, :], T.mp[:, :]).then_inc(S.lm, 16)
+        sca.dma_start(T.mapw[32:64, :], T.mp[:, :]).then_inc(S.lm, 16)
 
     ngi = 2
     imp = dict(allow_small_or_imprecise_dtypes=True)
@@ -141,18 +143,23 @@ def rank_program(g, core, T, topo):
         ofr = B if isA else A
         send(xfer([cores[r] for r in onr], T.ll[:, own], T.ll[:, own], REST, S.lan),
              xfer([cores[r] for r in ofr], T.ll[:, own], T.ll[:, own], OFF, S.laf))
-        for q in (g.sync, sca):
-            q.wait_ge(S.v, cnt["v"])
-        load_map(2)
-        load_map(3)
+        for u in range(2):
+            for k in range(2):
+                q = g.sync if k == 0 else sca
+                if u == 0:
+                    q.wait_ge(S.v, cnt["v"])
+                q.dma_start(T.mapw[64 + 32 * k + u:96 + 32 * k:2, 0:CX], T.mp[:, 8192 * u:8192 * u + CX]).then_inc(S.lm2, 16)
         g.sync.dma_start(T.win[:, tab0:tab0 + 2048], T.tab[:, 0:2048]).then_inc(S.lt0, 16)
         sca.dma_start(T.win[:, tab0 + 2048:tab0 + 4096], T.tab[:, 2048:4096]).then_inc(S.lt1, 16)
 
         def tables(c, to):
             sl = slice(tab0 + 2048 * c, tab0 + 2048 * c + 2048)
-            send(xfer(to, T.win[:, sl], T.win[:, sl], ALL, S["tc%d" % c]))
+            send(xfer([to], T.win[:, sl], T.win[:, sl], ALL, S["tc%d" % c]))
         g.wait_ge(S.lt0, 16)
-        tables(0, [cores[mate]] if isA else [HB[bi]])
+        tables(0, cores[mate] if isA else HB[bi])
+        if isB:
+            g.wait_ge(S.lt1, 16)
+            tables(1, HB[bi])
         vec.wait_ge(S.gi, ngi)
         ts(T.pa_i[:, 0:1], T.pio[:, 0:1], 1, OP.arith_shift_right, 15, OP.bitwise_and)
         ts(T.pa_i[:, 4:5], T.pio[:, 0:1], 1, OP.bitwise_and)
@@ -205,27 +212,38 @@ def rank_program(g, core, T, topo):
                                  T.ind[:, :], True, True)
             P(ins)
 
-        order = [rank] + onr + ofr
+        todo = list(range(CX, 8192, 2048))
+
+        def double():
+            if todo:
+                c0 = todo.pop(0)
+                cp(T.mapw[64:128, c0:c0 + 2048], T.mapw[0:64, c0:c0 + 2048])
+
         conv(rank)
         bcast(rank)
         onehot(rank, False)
+        vec.wait_ge(S.lm, 32)
+        double()
         vec.wait_ge(S.lan, len(bits(REST)) * len(onr))
         for r in onr:
             conv(r)
         for r in onr:
             bcast(r)
         for r in onr:
-            onehot(r, order.index(r) % 2 == 1)
+            onehot(r, True)
+        if isB:
+            double()
         vec.wait_ge(S.laf, len(bits(OFF)) * len(ofr))
         for r in ofr:
             conv(r)
         for r in ofr:
             bcast(r)
+        double()
         for r in ofr:
-            onehot(r, order.index(r) % 2 == 1)
-        vec.wait_ge(S.lm, 64)
+            onehot(r, r != ofr[-1])
+        vec.wait_ge(S.lm2, 64)
         vw()
-        for r in order:
+        for r in [rank] + onr + ofr:
             look(r)
         vec.wait_ge(S.p, cnt["p"])
         mine = slice(96 * rank, 96 * rank + 96)
@@ -233,50 +251,57 @@ def rank_program(g, core, T, topo):
         g.wait_ge(S.v, cnt["v"])
         send(xfer([cores[r] for r in onr] + (HB if isB else []), T.part[:, mine], T.part[:, mine], REST, S.pan),
              xfer([cores[r] for r in ofr] + (HB if isA else []), T.part[:, mine], T.part[:, mine], OFF, S.pan))
-        g.wait_ge(S.lt1, 16)
         if isA:
-            tables(1, [cores[mate]])
+            g.wait_ge(S.lt1, 16)
+            tables(1, cores[mate])
         else:
-            tables(1, [HB[bi], cores[B[1 - bi]]])
-            tables(0, [cores[B[1 - bi]]])
+            for c in range(2):
+                tables(c, cores[B[1 - bi]])
     else:
         k = HB.index(core)
         for c in range(2):
             sl = slice(4096 * k + 2048 * c, 4096 * k + 2048 * c + 2048)
-            g.wait_ge(S["tc%d" % c], len(bits(ALL)))
+            g.wait_ge(S["tc%d" % c], NALL)
             send(xfer([HB[1 - k]], T.win[:, sl], T.win[:, sl], ALL, S.tb))
         vec.wait_ge(S.gi, ngi)
 
     ts(T.ident[:, :], T.dio[:, :], 0.0, OP.is_equal)
-    for r in range(6):
+    for r in range(3 if isA else 1):
         ts(T.repm[:, 128 * r:128 * r + 128], T.eio[:, :], float(16 * r), OP.is_equal)
-
-    vec.wait_ge(S.pan, 8 * (len(cores) - (0 if rank is None else 1)))
-    vw()
-    tt(T.s3[:, :], T.part[:, 0:288], T.part[:, 288:576], OP.add)
-    vw()
-    tt(T.s2[:, :], T.s3[:, 0:96], T.s3[:, 96:192], OP.add)
-    vw()
-    tt(T.ci[:, :], T.s2[:, :], T.s3[:, 192:288], OP.add)
-    vw()
+    if rank is not None:
+        ts(W(1), T.bas[:, :], 8192.0, OP.add)
     if isA:
-        ts(T.e1[:, :], T.ci[:, :], 1, OP.arith_shift_right, 4096, OP.bitwise_and)
-        ts(T.e2[:, :], T.ci[:, :], 4095, OP.bitwise_and)
-        vw()
-        tt(T.loc[:, :], T.e1[:, :], T.e2[:, :], OP.add)
-    else:
-        ts(T.e2[:, :], T.ci[:, :], 8191, OP.bitwise_and)
-        vw()
-        cp(T.loc[:, :], T.e2[:, :])
+        ts(W(5), T.bas[:, :], float(-512 * h - 512), OP.add)
+        ts(W(8), T.bas[:, :], float(-512 * (2 + h)), OP.add)
 
-    def turn(src, rows, ps):
+    def add6(out, c0, n, at, fill=None):
+        x = [T.part[:, 96 * o + c0:96 * o + c0 + n] for o in range(6)]
+        z = [T.q[:, at + n * i:at + n * i + n] for i in range(4)]
+        for i in range(3):
+            tt(z[i], x[2 * i], x[2 * i + 1], OP.add)
+        if fill:
+            fill()
+        vw()
+        tt(z[3], z[0], z[1], OP.add)
+        vw()
+        tt(out, z[3], z[2], OP.add)
+        vw()
+
+    def turn(src, rows, ps, at):
         ten.wait_ge(S.v, cnt["v"])
-        return P(ten.matmul(ps[0:rows, 0:128], src, T.ident[:, :], True, True))
+        n = P(ten.matmul(ps[0:rows, 0:128], src, T.ident[:, :], True, True))
 
-    def spread(lt, rows, blocks, col):
-        for i, b in enumerate(blocks):
-            ins = ten.matmul(T.ps_s[:, col + 128 * i:col + 128 * i + 128], T.repm[0:rows, 128 * b:128 * b + 128],
-                             lt[0:rows, :], True, True)
+        def take():
+            vec.wait_ge(S.p, n)
+            cp(T.lt[0:rows, at:at + 128], ps[0:rows, 0:128])
+            ten.wait_ge(S.v, cnt["v"])
+        return take
+
+    def spread(at, rows, parts, col):
+        for b, m, n in parts:
+            ins = ten.matmul(T.ps_s[:, col:col + n], T.repm[0:rows, 128 * b:128 * b + 128],
+                             T.lt[0:rows, at + m:at + m + n], True, True)
+            col += n
         return P(ins)
 
     def store(c, n):
@@ -284,94 +309,101 @@ def rank_program(g, core, T, topo):
         q.wait_ge(S.v, n)
         q.dma_start(T.y[:, 512 * c:512 * c + 512], T.yo[:, 512 * c:512 * c + 512]).then_inc(S.st, 16)
 
-    n1 = turn(T.loc[:, :], 96, T.ps_t)
-    if rank is not None:
-        po = slice(16 * rank, 16 * rank + 16)
+    vec.wait_ge(S.pan, 8 * (len(cores) - (0 if rank is None else 1)))
+    vw()
     if isA:
-        lbn = B[pa]
-        pl = slice(16 * lbn, 16 * lbn + 16)
-        ts(T.par[:, :], T.ci[:, :], 12, OP.arith_shift_right, 1, OP.bitwise_and)
-        vec.wait_ge(S.p, n1)
-        cp(T.lt[0:96, :], T.ps_t[0:96, 0:128])
-        ten.wait_ge(S.v, cnt["v"])
-        nB = spread(T.lt, 96, B, 0)
-        nP = spread(T.lt, 96, [pt], 512)
+        bl = slice(64, 96)
+        add6(T.ci[:, bl], 64, 32, 0)
+        ts(T.e1[:, bl], T.ci[:, bl], 1, OP.arith_shift_right, 4096, OP.bitwise_and)
+        ts(T.e2[:, bl], T.ci[:, bl], 4095, OP.bitwise_and)
+        ts(T.hp[:, :], T.ci[:, pl], 3, OP.arith_shift_right, 512, OP.bitwise_and)
         vw()
-        ts(T.mis[:, :], T.par[:, :], float(pa), OP.not_equal)
-        vec.wait_ge(S.p, nB)
-        cp(T.ou[:, 0:256], T.ps_s[:, 0:256])
+        tt(T.loc[:, bl], T.e1[:, bl], T.e2[:, bl], OP.add)
+        tt(T.loc[:, 96:112], T.hp[:, :], W(8), OP.add)
+        take1 = turn(T.loc[:, 64:112], 48, T.ps_t, 0)
+        got = []
+
+        def fill():
+            take1()
+            got.append(spread(0, 48, [(0, 64 + 32 * h, 32), (1, 64 + 32 * h, 32), (pt & 1, 32 * h, 32), (2, 64 + 32 * h, 32)], 0))
+        al = slice(0, 64)
+        add6(T.ci[:, al], 0, 64, 128, fill)
+        vec.wait_ge(S.p, got[0])
+        nho = cp(T.ou[:, 0:128], T.ps_s[:, 0:128])
         for nm_, ct in (("lt0", 16), ("lt1", 16), ("tc0", 16), ("tc1", 16)):
             vec.wait_ge(S[nm_], ct)
         vw()
-        tw = slice(512, 8704)
-        for i, (l, m) in enumerate([(pt & 1, 32 * h), (0, 64 + 32 * h), (1, 64 + 32 * h)]):
-            cp(T.bco[:, 512 * i:512 * i + 512], T.win[:, tw].indirect(T.ou[:, 128 * l + m:128 * l + m + 32]))
-        g.wait_ge(S.v, cnt["v"])
-        ab = bits(ALL)
-        hw = slice(512 * pa, 512 * pa + 512)
-        send(xfer([cores[pt]], T.bco[:, 0:512], T.win[:, 0:512], tomask(ab[0:8]), S.lbm),
-             xfer([HA[2 * h]], T.bco[:, 512:1024], T.win[:, hw], tomask(ab[8:12]), S.hc),
-             xfer([HA[2 * h + 1]], T.bco[:, 1024:1536], T.win[:, hw], tomask(ab[12:16]), S.hc))
-        ts(T.isb[:, :], T.ci[:, po], 16384.0, OP.is_ge)
-        ts(T.w1[:, :], T.bas[:, :], 8192.0, OP.add)
-        ts(T.w5[:, :], T.bas[:, :], float(-512 * h - 512), OP.add)
-        ts(T.w8[:, :], T.par[:, pl], 512.0, OP.mult, float(-512 * (2 + h)), OP.add)
-        vw()
-        tt(T.f2[:, 32:48], T.w8[:, :], T.bas[:, :], OP.add)
-        tt(T.w6[:, :], T.w5[:, :], T.loc[:, pl], OP.subtract)
-        tt(T.w2[:, :], T.w1[:, :], T.loc[:, po], OP.subtract)
-        tt(T.w3[:, :], T.mis[:, po], T.isb[:, :], OP.max)
-        ts(T.w9[:, :], T.isb[:, :], 2048.0, OP.mult)
-        vw()
-        tt(T.w7[:, :], T.w6[:, :], T.mis[:, pl], OP.mult)
-        tt(T.w4[:, :], T.w2[:, :], T.w3[:, :], OP.mult)
-        ts(T.w5[:, :], T.loc[:, pl], 512.0, OP.add)
-        tt(T.w8[:, :], T.loc[:, po], T.w9[:, :], OP.add)
-        vw()
-        tt(T.f2[:, 16:32], T.w5[:, :], T.w7[:, :], OP.add)
-        tt(T.f2[:, 0:16], T.w8[:, :], T.w4[:, :], OP.add)
-        n2 = turn(T.f2[:, :], 48, T.ps_r)
-        vec.wait_ge(S.p, nP)
-        cp(T.ou[:, 256:384], T.ps_s[:, 512:640])
-        vec.wait_ge(S.p, n2)
-        cp(T.lt2[0:48, :], T.ps_r[0:48, 0:128])
-        ten.wait_ge(S.v, cnt["v"])
-        n3 = spread(T.lt2, 48, [0, 1, 2], 1024)
-        vw()
-        cp(T.sv[:, 0:1024], T.win[:, tw].indirect(T.ou[:, 256:320]))
-        vec.wait_ge(S.p, n3)
-        cp(T.o2[:, :], T.ps_s[:, 1024:1408])
-        vw()
-        nho = cp(T.hof[:, :], T.o2[:, 320 + 32 * h:352 + 32 * h])
-        cp(T.sv[:, 1024:2048], T.win[:, tw].indirect(T.ou[:, 320:384]))
-        vec.wait_ge(S.lbm, 8)
-        nm = cp(T.mgo[:, :], T.win[:, 0:8704].indirect(T.o2[:, 128 + 32 * h:160 + 32 * h]))
         g.wait_ge(S.v, nho)
-        send(xfer([HA[rank]], T.hof[:, :], T.hof[:, :], ALL, S.ho))
-        send(xfer([cores[pt]], T.sv[:, 0:1024], T.win[:, 8704:9728], ALL, S.lp))
+        send(xfer([HA[rank]], T.ou[:, 96:128], T.ou[:, 96:128], ALL, S.ho))
+        tw = slice(512, 8704)
+        hw = slice(512 * pa, 512 * pa + 512)
+        for i, (to, dst, sem) in enumerate([(HA[2 * h], hw, S.hc), (HA[2 * h + 1], hw, S.hc), (cores[pt], slice(0, 512), S.lbm)]):
+            sl = slice(512 * i, 512 * i + 512)
+            n = cp(T.bco[:, sl], T.win[:, tw].indirect(T.ou[:, 32 * i:32 * i + 32]))
+            g.wait_ge(S.v, n)
+            send(xfer([to], T.bco[:, sl], T.win[:, dst], ALL, sem))
+        ts(T.e1[:, al], T.ci[:, al], 1, OP.arith_shift_right, 4096, OP.bitwise_and)
+        ts(T.e2[:, al], T.ci[:, al], 4095, OP.bitwise_and)
+        ts(T.par[:, :], T.ci[:, :], 12, OP.arith_shift_right, 1, OP.bitwise_and)
+        tt(W(6), W(5), T.loc[:, pl], OP.subtract)
+        ts(W(10), T.loc[:, pl], 512.0, OP.add)
+        vw()
+        ts(T.mis[:, :], T.par[:, :], float(pa), OP.not_equal)
+        tt(T.loc[:, al], T.e1[:, al], T.e2[:, al], OP.add)
+        tt(W(12), T.e1[:, pp], T.e2[:, pp], OP.add)
+        vw()
+        tt(W(7), W(6), T.mis[:, pl], OP.mult)
+        vw()
+        tt(W(13), W(10), W(7), OP.add)
+        take2 = turn(T.w[:, 16 * 12:16 * 14], 32, T.ps_r, 128)
+        ts(W(0), T.ci[:, po], 16384.0, OP.is_ge)
+        tt(W(2), W(1), T.loc[:, po], OP.subtract)
+        take2()
+        n3 = spread(128, 32, [(0, 0, 128), (1, 32 * h, 32)], 512)
+        vw()
+        tt(W(3), T.mis[:, po], W(0), OP.max)
+        ts(W(9), W(0), 2048.0, OP.mult)
+        vw()
+        tt(W(4), W(2), W(3), OP.mult)
+        tt(W(11), T.loc[:, po], W(9), OP.add)
+        vec.wait_ge(S.p, n3)
+        cp(T.ou[:, 128:288], T.ps_s[:, 512:672])
+        vw()
+        tt(W(14), W(11), W(4), OP.add)
+        take3 = turn(W(14), 16, T.ps_t, 256)
+        ns0 = cp(T.sv[:, 0:1024], T.win[:, tw].indirect(T.ou[:, 128:192]))
+        vec.wait_ge(S.lbm, NALL)
+        nm = cp(T.mgo[:, :], T.win[:, 0:8704].indirect(T.ou[:, 256:288]))
+        ns1 = cp(T.sv[:, 1024:2048], T.win[:, tw].indirect(T.ou[:, 192:256]))
+        g.wait_ge(S.v, ns0)
+        send(xfer([cores[pt]], T.sv[:, 0:1024], T.win[:, 8704:9728], REST, S.lp))
         g.wait_ge(S.v, nm)
         c0 = 8192 + 512 * h
         send(xfer([cores[lbn]], T.mgo[:, :], T.win[:, c0:c0 + 512], OFF, S.m0))
-        send(xfer([cores[pt]], T.sv[:, 1024:2048], T.win[:, 9728:10752], ALL, S.lp))
-        vec.wait_ge(S.lp, 32)
+        g.wait_ge(S.v, ns1)
+        send(xfer([cores[pt]], T.sv[:, 1024:2048], T.win[:, 9728:10752], REST, S.lp))
+        take3()
+        vec.wait_ge(S.p, spread(256, 16, [(0, 0, 128)], 1024))
+        cp(T.ou[:, 288:416], T.ps_s[:, 1024:1152])
+        vw()
+        vec.wait_ge(S.lp, 16)
         for c in range(4):
             vec.wait_ge(S["lsv%d" % c], 8)
             store(c, cp(T.yo[:, 512 * c:512 * c + 512],
-                        T.win[:, 512:11264 + 512 * c].indirect(T.o2[:, 32 * c:32 * c + 32])))
+                        T.win[:, 512:11264 + 512 * c].indirect(T.ou[:, 288 + 32 * c:320 + 32 * c])))
     else:
         s = B.index(rank) if isB else 2 + HB.index(core)
-        vec.wait_ge(S.p, n1)
-        cp(T.lt[0:96, :], T.ps_t[0:96, 0:128])
-        ten.wait_ge(S.v, cnt["v"])
-        vec.wait_ge(S.p, spread(T.lt, 96, [A[s]], 0))
-        cp(T.ou[:, 0:128], T.ps_s[:, 0:128])
+        add6(W(2), 16 * A[s], 16, 0)
+        turn(W(2), 16, T.ps_t, 0)()
+        vec.wait_ge(S.p, spread(0, 16, [(0, 0, 128)], 0))
+        ts(T.ou[:, 0:128], T.ps_s[:, 0:128], -16384.0, OP.add, 0.0, OP.max)
         if isB:
             vec.wait_ge(S.lt0, 16)
             vec.wait_ge(S.lt1, 16)
         else:
-            vec.wait_ge(S.tb, 32)
-        vec.wait_ge(S.tc0, 16)
-        vec.wait_ge(S.tc1, 16)
+            vec.wait_ge(S.tb, 2 * NALL)
+        vec.wait_ge(S.tc0, NALL)
+        vec.wait_ge(S.tc1, NALL)
         vw()
         for c in range(4):
             sc = slice(512 * c, 512 * c + 512)
@@ -379,26 +411,24 @@ def rank_program(g, core, T, topo):
             g.wait_ge(S.v, n)
             send(xfer([cores[A[s]]], T.sv[:, sc], T.win[:, 10752 + 512 * c:11264 + 512 * c], OFF, S["lsv%d" % c]))
         if isB:
-            ts(T.isb[:, :], T.ci[:, po], 16384.0, OP.is_ge)
-            ts(T.w1[:, :], T.bas[:, :], 8192.0, OP.add)
+            add6(W(3), 16 * rank, 16, 128)
+            ts(W(0), W(3), 16384.0, OP.is_ge)
+            ts(W(10), W(3), -16384.0, OP.add)
             vw()
-            tt(T.w2[:, :], T.loc[:, po], T.w1[:, :], OP.subtract)
+            tt(W(4), W(10), W(1), OP.subtract)
             vw()
-            tt(T.w3[:, :], T.w2[:, :], T.isb[:, :], OP.mult)
+            tt(W(5), W(4), W(0), OP.mult)
             vw()
-            tt(T.f2[:, 0:16], T.w3[:, :], T.w1[:, :], OP.add)
-            n2 = turn(T.f2[:, 0:16], 16, T.ps_r)
-            vec.wait_ge(S.p, n2)
-            cp(T.lt2[0:16, :], T.ps_r[0:16, 0:128])
-            ten.wait_ge(S.v, cnt["v"])
-            vec.wait_ge(S.p, spread(T.lt2, 16, [0], 1024))
-            cp(T.o2[:, 0:128], T.ps_s[:, 1024:1152])
+            tt(W(12), W(5), W(1), OP.add)
+            turn(W(12), 16, T.ps_r, 128)()
+            vec.wait_ge(S.p, spread(128, 16, [(0, 0, 128)], 1024))
+            cp(T.ou[:, 288:416], T.ps_s[:, 1024:1152])
             vw()
             for c in range(4):
                 if c % 2 == 0:
                     vec.wait_ge(S["m%d" % (c // 2)], 16)
                 w = 9216 if c < 2 else 10240
-                store(c, cp(T.yo[:, 512 * c:512 * c + 512], T.win[:, 0:w].indirect(T.o2[:, 32 * c:32 * c + 32])))
+                store(c, cp(T.yo[:, 512 * c:512 * c + 512], T.win[:, 0:w].indirect(T.ou[:, 288 + 32 * c:320 + 32 * c])))
     if rank is not None:
         g.wait_ge(S.st, 64)
     g.wait_ge(S.v, cnt["v"])

from concourse.bass import DstId, RemoteDMATransfer
from concourse.mybir import AluOpType, ActivationFunctionType

OP = AluOpType
ACT = ActivationFunctionType
SIM = 256
_F, _I, _U, _H = "float32", "int32", "uint16", "bfloat16"
_SB = [("idxi", 32, _I), ("ti", 64, _I), ("si", 32, _I), ("lf", 64, _F), ("ll", 384, _F), ("lu", 192, _U), ("lb", 192, _H),
       ("mapw", 8192, _I), ("win", 12800, _F), ("bio", 128, _H), ("lsel", 2048, _H), ("dio", 128, _F), ("eio", 128, _F),
       ("pio", 4, _I), ("rio", 4, _I), ("bas", 16, _F), ("pa_i", 8, _I), ("pcs", 4, _F), ("npc", 4, _F), ("ri5", 4, _I),
       ("ind", 4, _F), ("ident", 128, _F), ("repm", 384, _F), ("absb", 3072, _F), ("mask", 3072, _H), ("mg", 3072, _F),
       ("part", 576, _F), ("q", 512, _F), ("ci", 96, _I), ("e1", 96, _I), ("e2", 96, _I),
       ("loc", 112, _F), ("hp", 16, _I), ("par", 96, _I), ("mis", 96, _F), ("lt", 384, _F), ("ou", 512, _U),
       ("bco", 1536, _F), ("sv", 2048, _F), ("mgo", 512, _F), ("yo", 2048, _F), ("w", 256, _F)]
SCRATCH = {n: ("sbuf", [128, w], d) for n, w, d in _SB}
SCRATCH.update({"ps_s": ("psum", [128, 3072], _F), "ps_r": ("psum", [128, 512], _F), "ps_t": ("psum", [128, 512], _F)})
SEMAPHORES = ["v", "p", "s", "gi", "li", "lm", "lm2", "lt0", "lt1", "lan", "laf", "pan", "lsm", "tb", "tc0", "tc1",
              "lbm", "hc", "ho", "lp", "lsv0", "lsv1", "lsv2", "lsv3", "m0", "m1", "st"]


def rank_program(g, core, T, topo):
    S = T.sem
    cores = list(T.cores)
    rank = T.rank_of(core)

    def place(c):
        return (topo.host(c), topo.chip(c))

    A = [r for r in range(len(cores)) if place(cores[r]) == place(cores[0])]
    B = [r for r in range(len(cores)) if r not in A]
    HA = [c for c in range(SIM) if place(c) == place(cores[A[0]]) and topo.die(c) != topo.die(cores[A[0]])][:4]
    HB = [c for c in range(SIM) if place(c) == place(cores[B[0]]) and topo.die(c) != topo.die(cores[B[0]])][:2]
    if rank is None and core not in HA and core not in HB:
        return

    def bits(m):
        return [b for b in range(16) if (m >> b) & 1]

    onA = place(core) == place(cores[A[0]])
    near = [cores[r] for r in (A if onA else B) if cores[r] != core][0]
    ALL = topo.mask(core, near)
    OFF = topo.mask(core, cores[B[0]] if onA else cores[A[0]])
    REST = ALL & ~OFF
    NALL = len(bits(ALL))
    cnt = {"v": 0, "p": 0, "s": 0, "ls": 0}
    vec, ten, sca = g.vector, g.tensor, g.scalar

    def V(ins):
        ins.then_inc(S.v, 1)
        cnt["v"] += 1
        return cnt["v"]

    def P(ins):
        ins.then_inc(S.p, 1)
        cnt["p"] += 1
        return cnt["p"]

    def vw():
        vec.wait_ge(S.v, cnt["v"])

    def ts(out, a, s1, op, s2=None, op2=None):
        if op2 is None:
            return V(vec.tensor_scalar(out, a, s1, None, op))
        return V(vec.tensor_scalar(out, a, s1, s2, op, op2))

    def tt(out, a, b, op):
        return V(vec.tensor_tensor(out, a, b, op))

    def cp(out, a):
        return V(vec.tensor_copy(out, a))

    def W(n):
        return T.w[:, 16 * n:16 * n + 16]

    def xfer(dests, src, dst, mask, sem):
        ids = []
        for d in dests:
            rid, pid = topo.addr(d, core)
            ids.append(DstId(rid=rid, pnc=pid))
        cnt["ls"] += len(bits(mask))
        return RemoteDMATransfer(dst_ids=ids, dma_engine_mask=mask, remote_sem=sem, srcs=[src], dsts=[dst] * len(ids), alu_op=0)

    def send(*trs):
        g.remote_dma_fused(list(trs), local_sem=S.lsm)

    if core in HA:
        k = HA.index(core)
        e, h = k & 1, k >> 1
        vec.wait_ge(S.ho, NALL)
        vec.wait_ge(S.hc, 2 * NALL)
        n = cp(T.mgo[:, :], T.win[:, 0:1024].indirect(T.ou[:, 96:128]))
        g.wait_ge(S.v, n)
        c0 = 8192 + 512 * (2 + h)
        send(xfer([cores[B[e]]], T.mgo[:, :], T.win[:, c0:c0 + 512], OFF, S.m1))
        g.wait_ge(S.lsm, cnt["ls"])
        return

    isA = rank is not None and rank in A
    isB = rank is not None and rank in B
    CX = 4096 if isA else 2048
    if isA:
        pa, h, pt, mate = rank & 1, rank >> 1, rank ^ 1, rank ^ 2
        tab0 = 512 + 4096 * h
        lbn = B[pa]
        pl = slice(16 * lbn, 16 * lbn + 16)
        pp = slice(16 * pt, 16 * pt + 16)
    elif isB:
        bi = B.index(rank)
        tab0 = 4096 * bi
    if rank is not None:
        po = slice(16 * rank, 16 * rank + 16)

    if rank is not None:
        g.sync.dma_start(T.idxi[:, 0:16], T.idx[:, :]).then_inc(S.li, 16)
        sca.dma_start(T.idxi[:, 16:32], T.idx[:, :]).then_inc(S.li, 16)
        g.sync.dma_start(T.mapw[0:32, :], T.mp[:, :]).then_inc(S.lm, 16)
        sca.dma_start(T.mapw[32:64, :], T.mp[:, :]).then_inc(S.lm, 16)

    ngi = 2
    imp = dict(allow_small_or_imprecise_dtypes=True)
    if rank is not None:
        g.iota(T.bio[:, :], [[-32, 4], [0, 32]], 0, 1, **imp).then_inc(S.gi, 1)
        g.iota(T.pio[:, 0:1], [[1, 1]], 0, 1).then_inc(S.gi, 1)
        g.iota(T.rio[:, :], [[-32, 4]], 0, 1).then_inc(S.gi, 1)
        g.iota(T.bas[:, :], [[1, 16]], 0, 16, **imp).then_inc(S.gi, 1)
        ngi += 4
    g.iota(T.dio[:, :], [[-1, 128]], 0, 1, **imp).then_inc(S.gi, 1)
    g.iota(T.eio[:, :], [[0, 8], [-1, 16]], 0, 1, **imp).then_inc(S.gi, 1)

    if rank is not None:
        vec.wait_ge(S.li, 32)
        ts(T.ti[:, 0:32], T.idxi[:, :], 4, OP.arith_shift_right, 8191, OP.bitwise_and)
        ts(T.si[:, :], T.idxi[:, :], 15, OP.bitwise_and)
        ts(T.ti[:, 32:64], T.idxi[:, :], 13, OP.arith_shift_right, 0xFFFFF0, OP.bitwise_and)
        vw()
        cp(T.lf[:, 0:32], T.ti[:, 0:32])
        tt(T.lf[:, 32:64], T.si[:, :], T.ti[:, 32:64], OP.add)
        vw()
        own = slice(64 * rank, 64 * rank + 64)
        V(vec.transpose(T.ll[:, own], T.lf[:, :]))
        g.wait_ge(S.v, cnt["v"])
        onr = [r for r in (A if isA else B) if r != rank]
        ofr = B if isA else A
        send(xfer([cores[r] for r in onr], T.ll[:, own], T.ll[:, own], REST, S.lan),
             xfer([cores[r] for r in ofr], T.ll[:, own], T.ll[:, own], OFF, S.laf))
        for u in range(2):
            for k in range(2):
                q = g.sync if k == 0 else sca
                if u == 0:
                    q.wait_ge(S.v, cnt["v"])
                q.dma_start(T.mapw[64 + 32 * k + u:96 + 32 * k:2, 0:CX], T.mp[:, 8192 * u:8192 * u + CX]).then_inc(S.lm2, 16)
        g.sync.dma_start(T.win[:, tab0:tab0 + 2048], T.tab[:, 0:2048]).then_inc(S.lt0, 16)
        sca.dma_start(T.win[:, tab0 + 2048:tab0 + 4096], T.tab[:, 2048:4096]).then_inc(S.lt1, 16)

        def tables(c, to):
            sl = slice(tab0 + 2048 * c, tab0 + 2048 * c + 2048)
            send(xfer([to], T.win[:, sl], T.win[:, sl], ALL, S["tc%d" % c]))
        g.wait_ge(S.lt0, 16)
        tables(0, cores[mate] if isA else HB[bi])
        if isB:
            g.wait_ge(S.lt1, 16)
            tables(1, HB[bi])
        vec.wait_ge(S.gi, ngi)
        ts(T.pa_i[:, 0:1], T.pio[:, 0:1], 1, OP.arith_shift_right, 15, OP.bitwise_and)
        ts(T.pa_i[:, 4:5], T.pio[:, 0:1], 1, OP.bitwise_and)
        ts(T.ri5[:, :], T.rio[:, :], 5, OP.arith_shift_right)
        vw()
        ts(T.pcs[:, 1:2], T.pa_i[:, 4:5], 16.0, OP.mult, float(32 * rank), OP.add)
        ts(T.ind[:, :], T.ri5[:, :], 0.0, OP.is_equal)
        vw()
        tt(T.pcs[:, 0:1], T.pa_i[:, 0:1], T.pcs[:, 1:2], OP.add)
        vw()
        ts(T.npc[:, 0:1], T.pcs[:, 0:1], -1.0, OP.mult)
        for x in range(16):
            ts(T.lsel[:, 128 * x:128 * x + 128], T.bio[:, :], float(x), OP.is_equal)

        vc, pb, ms = {}, {}, {}

        def conv(r):
            cp(T.lb[:, 32 * r:32 * r + 32], T.ll[:, 64 * r + 32:64 * r + 64])
            vc[r] = cp(T.lu[:, 32 * r:32 * r + 32], T.ll[:, 64 * r:64 * r + 32])

        def bcast(r):
            ten.wait_ge(S.v, vc[r])
            for x in range(16):
                ins = ten.matmul(T.ps_s[:, 512 * r + x:512 * r + 512:16], T.lsel[:, 128 * x:128 * x + 128],
                                 T.lb[:, 32 * r:32 * r + 32], True, True)
            pb[r] = P(ins)

        def onehot(r, on_scalar):
            b = slice(512 * r, 512 * r + 512)
            if on_scalar:
                sca.wait_ge(S.p, pb[r])
                sca.wait_ge(S.v, vc[r])
                sca.activation(T.absb[:, b], T.ps_s[:, b], ACT.Abs, bias=T.npc[:, 0:1], scale=1.0).then_inc(S.s, 1)
                sca.wait_ge(S.s, cnt["s"] + 1)
                sca.activation(T.mask[:, b], T.absb[:, b], ACT.Relu, bias=1.0, scale=-1.0).then_inc(S.s, 1)
                cnt["s"] += 2
                ms[r] = cnt["s"]
            else:
                vec.wait_ge(S.p, pb[r])
                ts(T.mask[:, b], T.ps_s[:, b], T.pcs[:, 0:1], OP.is_equal)

        def look(r):
            b = slice(512 * r, 512 * r + 512)
            if r in ms:
                vec.wait_ge(S.s, ms[r])
            n = tt(T.mg[:, b], T.mapw[:, :].indirect(T.lu[:, 32 * r:32 * r + 32]), T.mask[:, b], OP.mult)
            ten.wait_ge(S.v, n)
            for bb in range(4):
                ins = ten.matmul(T.ps_r[:, 16 * r + bb:16 * r + 16:4], T.mg[:, 512 * r + 128 * bb:512 * r + 128 * bb + 128],
                                 T.ind[:, :], True, True)
            P(ins)

        todo = list(range(CX, 8192, 2048))

        def double():
            if todo:
                c0 = todo.pop(0)
                cp(T.mapw[64:128, c0:c0 + 2048], T.mapw[0:64, c0:c0 + 2048])

        conv(rank)
        bcast(rank)
        onehot(rank, False)
        vec.wait_ge(S.lm, 32)
        double()
        vec.wait_ge(S.lan, len(bits(REST)) * len(onr))
        for r in onr:
            conv(r)
        for r in onr:
            bcast(r)
        for r in onr:
            onehot(r, True)
        if isB:
            double()
        vec.wait_ge(S.laf, len(bits(OFF)) * len(ofr))
        for r in ofr:
            conv(r)
        for r in ofr:
            bcast(r)
        double()
        for r in ofr:
            onehot(r, r != ofr[-1])
        vec.wait_ge(S.lm2, 64)
        vw()
        for r in [rank] + onr + ofr:
            look(r)
        vec.wait_ge(S.p, cnt["p"])
        mine = slice(96 * rank, 96 * rank + 96)
        cp(T.part[:, mine], T.ps_r[:, 0:96])
        g.wait_ge(S.v, cnt["v"])
        send(xfer([cores[r] for r in onr] + (HB if isB else []), T.part[:, mine], T.part[:, mine], REST, S.pan),
             xfer([cores[r] for r in ofr] + (HB if isA else []), T.part[:, mine], T.part[:, mine], OFF, S.pan))
        if isA:
            g.wait_ge(S.lt1, 16)
            tables(1, cores[mate])
        else:
            for c in range(2):
                tables(c, cores[B[1 - bi]])
    else:
        k = HB.index(core)
        for c in range(2):
            sl = slice(4096 * k + 2048 * c, 4096 * k + 2048 * c + 2048)
            g.wait_ge(S["tc%d" % c], NALL)
            send(xfer([HB[1 - k]], T.win[:, sl], T.win[:, sl], ALL, S.tb))
        vec.wait_ge(S.gi, ngi)

    ts(T.ident[:, :], T.dio[:, :], 0.0, OP.is_equal)
    for r in range(3 if isA else 1):
        ts(T.repm[:, 128 * r:128 * r + 128], T.eio[:, :], float(16 * r), OP.is_equal)
    if rank is not None:
        ts(W(1), T.bas[:, :], 8192.0, OP.add)
    if isA:
        ts(W(5), T.bas[:, :], float(-512 * h - 512), OP.add)
        ts(W(8), T.bas[:, :], float(-512 * (2 + h)), OP.add)

    def add6(out, c0, n, at, fill=None):
        x = [T.part[:, 96 * o + c0:96 * o + c0 + n] for o in range(6)]
        z = [T.q[:, at + n * i:at + n * i + n] for i in range(4)]
        for i in range(3):
            tt(z[i], x[2 * i], x[2 * i + 1], OP.add)
        if fill:
            fill()
        vw()
        tt(z[3], z[0], z[1], OP.add)
        vw()
        tt(out, z[3], z[2], OP.add)
        vw()

    def turn(src, rows, ps, at):
        ten.wait_ge(S.v, cnt["v"])
        n = P(ten.matmul(ps[0:rows, 0:128], src, T.ident[:, :], True, True))

        def take():
            vec.wait_ge(S.p, n)
            cp(T.lt[0:rows, at:at + 128], ps[0:rows, 0:128])
            ten.wait_ge(S.v, cnt["v"])
        return take

    def spread(at, rows, parts, col):
        for b, m, n in parts:
            ins = ten.matmul(T.ps_s[:, col:col + n], T.repm[0:rows, 128 * b:128 * b + 128],
                             T.lt[0:rows, at + m:at + m + n], True, True)
            col += n
        return P(ins)

    def store(c, n):
        q = g.sync if c % 2 == 0 else sca
        q.wait_ge(S.v, n)
        q.dma_start(T.y[:, 512 * c:512 * c + 512], T.yo[:, 512 * c:512 * c + 512]).then_inc(S.st, 16)

    vec.wait_ge(S.pan, 8 * (len(cores) - (0 if rank is None else 1)))
    vw()
    if isA:
        bl = slice(64, 96)
        add6(T.ci[:, bl], 64, 32, 0)
        ts(T.e1[:, bl], T.ci[:, bl], 1, OP.arith_shift_right, 4096, OP.bitwise_and)
        ts(T.e2[:, bl], T.ci[:, bl], 4095, OP.bitwise_and)
        ts(T.hp[:, :], T.ci[:, pl], 3, OP.arith_shift_right, 512, OP.bitwise_and)
        vw()
        tt(T.loc[:, bl], T.e1[:, bl], T.e2[:, bl], OP.add)
        tt(T.loc[:, 96:112], T.hp[:, :], W(8), OP.add)
        take1 = turn(T.loc[:, 64:112], 48, T.ps_t, 0)
        got = []

        def fill():
            take1()
            got.append(spread(0, 48, [(0, 64 + 32 * h, 32), (1, 64 + 32 * h, 32), (pt & 1, 32 * h, 32), (2, 64 + 32 * h, 32)], 0))
        al = slice(0, 64)
        add6(T.ci[:, al], 0, 64, 128, fill)
        vec.wait_ge(S.p, got[0])
        nho = cp(T.ou[:, 0:128], T.ps_s[:, 0:128])
        for nm_, ct in (("lt0", 16), ("lt1", 16), ("tc0", 16), ("tc1", 16)):
            vec.wait_ge(S[nm_], ct)
        vw()
        g.wait_ge(S.v, nho)
        send(xfer([HA[rank]], T.ou[:, 96:128], T.ou[:, 96:128], ALL, S.ho))
        tw = slice(512, 8704)
        hw = slice(512 * pa, 512 * pa + 512)
        for i, (to, dst, sem) in enumerate([(HA[2 * h], hw, S.hc), (HA[2 * h + 1], hw, S.hc), (cores[pt], slice(0, 512), S.lbm)]):
            sl = slice(512 * i, 512 * i + 512)
            n = cp(T.bco[:, sl], T.win[:, tw].indirect(T.ou[:, 32 * i:32 * i + 32]))
            g.wait_ge(S.v, n)
            send(xfer([to], T.bco[:, sl], T.win[:, dst], ALL, sem))
        ts(T.e1[:, al], T.ci[:, al], 1, OP.arith_shift_right, 4096, OP.bitwise_and)
        ts(T.e2[:, al], T.ci[:, al], 4095, OP.bitwise_and)
        ts(T.par[:, :], T.ci[:, :], 12, OP.arith_shift_right, 1, OP.bitwise_and)
        tt(W(6), W(5), T.loc[:, pl], OP.subtract)
        ts(W(10), T.loc[:, pl], 512.0, OP.add)
        vw()
        ts(T.mis[:, :], T.par[:, :], float(pa), OP.not_equal)
        tt(T.loc[:, al], T.e1[:, al], T.e2[:, al], OP.add)
        tt(W(12), T.e1[:, pp], T.e2[:, pp], OP.add)
        vw()
        tt(W(7), W(6), T.mis[:, pl], OP.mult)
        vw()
        tt(W(13), W(10), W(7), OP.add)
        take2 = turn(T.w[:, 16 * 12:16 * 14], 32, T.ps_r, 128)
        ts(W(0), T.ci[:, po], 16384.0, OP.is_ge)
        tt(W(2), W(1), T.loc[:, po], OP.subtract)
        take2()
        n3 = spread(128, 32, [(0, 0, 128), (1, 32 * h, 32)], 512)
        vw()
        tt(W(3), T.mis[:, po], W(0), OP.max)
        ts(W(9), W(0), 2048.0, OP.mult)
        vw()
        tt(W(4), W(2), W(3), OP.mult)
        tt(W(11), T.loc[:, po], W(9), OP.add)
        vec.wait_ge(S.p, n3)
        cp(T.ou[:, 128:288], T.ps_s[:, 512:672])
        vw()
        tt(W(14), W(11), W(4), OP.add)
        take3 = turn(W(14), 16, T.ps_t, 256)
        ns0 = cp(T.sv[:, 0:1024], T.win[:, tw].indirect(T.ou[:, 128:192]))
        vec.wait_ge(S.lbm, NALL)
        nm = cp(T.mgo[:, :], T.win[:, 0:8704].indirect(T.ou[:, 256:288]))
        ns1 = cp(T.sv[:, 1024:2048], T.win[:, tw].indirect(T.ou[:, 192:256]))
        g.wait_ge(S.v, ns0)
        send(xfer([cores[pt]], T.sv[:, 0:1024], T.win[:, 8704:9728], REST, S.lp))
        g.wait_ge(S.v, nm)
        c0 = 8192 + 512 * h
        send(xfer([cores[lbn]], T.mgo[:, :], T.win[:, c0:c0 + 512], OFF, S.m0))
        g.wait_ge(S.v, ns1)
        send(xfer([cores[pt]], T.sv[:, 1024:2048], T.win[:, 9728:10752], REST, S.lp))
        take3()
        vec.wait_ge(S.p, spread(256, 16, [(0, 0, 128)], 1024))
        cp(T.ou[:, 288:416], T.ps_s[:, 1024:1152])
        vw()
        vec.wait_ge(S.lp, 16)
        for c in range(4):
            vec.wait_ge(S["lsv%d" % c], 8)
            store(c, cp(T.yo[:, 512 * c:512 * c + 512],
                        T.win[:, 512:11264 + 512 * c].indirect(T.ou[:, 288 + 32 * c:320 + 32 * c])))
    else:
        s = B.index(rank) if isB else 2 + HB.index(core)
        add6(W(2), 16 * A[s], 16, 0)
        turn(W(2), 16, T.ps_t, 0)()
        vec.wait_ge(S.p, spread(0, 16, [(0, 0, 128)], 0))
        ts(T.ou[:, 0:128], T.ps_s[:, 0:128], -16384.0, OP.add, 0.0, OP.max)
        if isB:
            vec.wait_ge(S.lt0, 16)
            vec.wait_ge(S.lt1, 16)
        else:
            vec.wait_ge(S.tb, 2 * NALL)
        vec.wait_ge(S.tc0, NALL)
        vec.wait_ge(S.tc1, NALL)
        vw()
        for c in range(4):
            sc = slice(512 * c, 512 * c + 512)
            n = cp(T.sv[:, sc], T.win[:, 0:8192].indirect(T.ou[:, 32 * c:32 * c + 32]))
            g.wait_ge(S.v, n)
            send(xfer([cores[A[s]]], T.sv[:, sc], T.win[:, 10752 + 512 * c:11264 + 512 * c], OFF, S["lsv%d" % c]))
        if isB:
            add6(W(3), 16 * rank, 16, 128)
            ts(W(0), W(3), 16384.0, OP.is_ge)
            ts(W(10), W(3), -16384.0, OP.add)
            vw()
            tt(W(4), W(10), W(1), OP.subtract)
            vw()
            tt(W(5), W(4), W(0), OP.mult)
            vw()
            tt(W(12), W(5), W(1), OP.add)
            turn(W(12), 16, T.ps_r, 128)()
            vec.wait_ge(S.p, spread(128, 16, [(0, 0, 128)], 1024))
            cp(T.ou[:, 288:416], T.ps_s[:, 1024:1152])
            vw()
            for c in range(4):
                if c % 2 == 0:
                    vec.wait_ge(S["m%d" % (c // 2)], 16)
                w = 9216 if c < 2 else 10240
                store(c, cp(T.yo[:, 512 * c:512 * c + 512], T.win[:, 0:w].indirect(T.ou[:, 288 + 32 * c:320 + 32 * c])))
    if rank is not None:
        g.wait_ge(S.st, 64)
    g.wait_ge(S.v, cnt["v"])
    g.wait_ge(S.lsm, cnt["ls"])
